import numpy as np, ml_dtypes
CORES = [2,6,10,14,18,22,26,30]
N = 8
import mx_ref
BF = ml_dtypes.bfloat16
def gentries(a):
    return np.ascontiguousarray(a.reshape(8, 16, -1).transpose(0, 2, 1)).reshape(8, -1)
def gtable(e):
    e = np.asarray(e); return np.ascontiguousarray(e.reshape(8, -1, 16).transpose(0, 2, 1)).reshape(128, -1).astype(np.int32)
def gcols(t, e):
    v = np.concatenate([t.reshape(8, 16, -1, 4), np.zeros((8, 16, 1, 4), BF)], axis=2)
    return np.ascontiguousarray(np.stack([v[g][:, e[g]] for g in range(8)])).reshape(128, -1)
def tile(rs):
    return np.stack(rs, axis=2).reshape(128, -1).astype(BF)
def pick(q, e):
    c = np.concatenate([q[0].reshape(128, -1, 4), np.zeros((128, 1, 4), np.uint8)], axis=1); s = np.concatenate([q[1], np.ones((16, 1), np.uint8)], axis=1)
    return (np.ascontiguousarray(c[:, e].reshape(128, -1)), np.ascontiguousarray(s[:, e]))
def join(*qs):
    return (np.concatenate([q[0] for q in qs], axis=1), np.concatenate([q[1] for q in qs], axis=1))
def put(q, e, v):
    c, s = q[0].reshape(128, -1, 4).copy(), q[1].copy(); c[:, e] = v[0].reshape(128, -1, 4); s[:, e] = v[1]
    return (c.reshape(128, -1), s)
def pk(c, s):
    return (np.ascontiguousarray(c), mx_ref.live(s))
def emit(q):
    return q[0], q[1]
def packed(v, rng):
    q = [mx_ref.quantize(np.ascontiguousarray(v[r])) for r in range(N)]
    return np.stack([a for a, b in q]), np.stack([mx_ref.plane(b, rng) for a, b in q])
def values_of_codes():
    e, c = np.zeros((128, 128, 4), np.float32), np.zeros((128, 2, 4), np.uint8)
    e[np.arange(128), np.arange(128), 0] = 1
    c[:127, :, 0] = np.arange(256).reshape(2, 128).T[:127]
    return mx_ref.matmul(mx_ref.quantize(e.reshape(128, 512).astype(BF)), (c.reshape(128, 8), np.full((16, 2), 127, np.uint8))).T.reshape(-1).astype(np.float64)
CODE_VALUE, SCALE_VALUE = values_of_codes(), 2.0 ** (np.arange(256) - 127.0)
def decode(q):
    return (CODE_VALUE[q[0]].reshape(16, 8, -1, 4) * SCALE_VALUE[q[1]][:, None, :, None] + 0.0).reshape(128, -1).astype(np.float32)
def f(rng, *shape):
    return mx_ref.flush((rng.standard_normal(shape, dtype=np.float32) * np.exp2(rng.integers(-2, 3, shape[:-1] + (1,)))).astype(BF))
def wide(rng, *shape, cols=0):
    v = rng.standard_normal(shape, dtype=np.float32) * np.exp2(rng.integers(-12, 13, shape)).astype(np.float32)
    if cols: v *= np.repeat(np.exp2(rng.integers(-cols, cols + 1, shape[:-2] + (1, shape[-1] // 4))) * (rng.random(shape[:-2] + (1, shape[-1] // 4)) > 0.0625), 4, axis=-1).astype(np.float32)
    return mx_ref.flush(v.astype(BF))
C, L, S, R = 256, 32, 16, 3
G = np.arange(8)[:, None]
def big(v):
    v = v.astype(np.float32)
    v[np.abs(v) < np.float32(2.0 ** -16)] = 0
    return v.astype(BF)
def numbers_of(rng):
    u = np.array(f(rng, N, 128, 512)).reshape(N, 8, 16, 128, 4)
    for g in range(8):
        u[:, :g, :, 16 * g] = 0
        u[:, g + 1:, :, 16 * g] = 0
    return {"x": big(f(rng, N, 128, 4 * C)), "u": u.reshape(N, 128, 512), "v": np.array(f(rng, N, 128, 512))}
def layers(rng):
    return big(f(rng, N, 128, 2048)).reshape(N, 8, 16, 4, 8, 16, 4)
def weights(rng, w):
    c, p = packed(np.ascontiguousarray(w).reshape(N, 128, 2048), rng)
    return {"wc": c, "ws": p}
def routes(rng):
    return np.argsort(rng.random((N, 8, 2 * C)), axis=2) % C
def walks(rng):
    return rng.integers(0, C, (N, 8, C))
def ways(e, w):
    return {"rt": np.stack([gtable(a) for a in e]), "ft": np.stack([gtable(a) for a in w])}
def setup_inputs(rng):
    return {**numbers_of(rng), **weights(rng, layers(rng)), **ways(routes(rng), walks(rng))}
def setup_inputs_ties(rng):
    d = numbers_of(rng)
    e = rng.permutation(N)
    x = d["x"].reshape(N, 8, 16, C, 4)
    a = x[0][:, :8, :3].copy()
    a[:, :, 2] = 0
    for r in range(N):
        k = rng.permutation(C) % 3
        if r == e[0]: k = np.zeros(C, int)
        if r == e[1]: k = np.full(C, 2)
        x[r][:, :8] = a[:, :, k]
    u = d["u"].reshape(N, 8, 16, 128, 4)
    u[:, :, 8:, ::16] = 0
    w = layers(rng)
    w[:, :, :, :, :, :8] = 0
    return {"x": x.reshape(N, 128, 4 * C), "u": u.reshape(N, 128, 512), "v": d["v"], **weights(rng, w), **ways(routes(rng), walks(rng))}
def setup_inputs_near(rng):
    d = numbers_of(rng)
    x = np.zeros((N, 8, 16, C, 4), np.float32)
    u = d["u"].reshape(N, 128, 128, 4)
    u[:, :, ::16] = 0
    o, c = rng.permutation(N) % 4, rng.permutation(8) % 2 * 2.0 - 1.0
    e = np.zeros((N, 8, 2 * C), int)
    for r in range(N):
        i = (np.arange(C) + rng.integers(0, C, (8, 1))) % C
        e[r, :, :C] = np.argsort(i, axis=1)
        e[r, :, C:] = np.argsort(rng.random((8, C)), axis=1)
        size = 1.0 if o[r] < 2 else 2.0 ** -4
        z = (((i // 2)[:, :, None] >> np.arange(8)) & 1) * np.exp2(np.arange(8) - 23.0) * size
        x[r, :, 0, :, 0] = c[:, None] * (1 - r % 2 * 2) if o[r] < 2 else (8 + i % 2) * 2.0 ** -30
        x[r, :, 8] = z[:, :, :4]
        x[r, :, 9] = z[:, :, 4:]
        x[r, :, 10:] = rng.integers(4, 8, (8, 6, C, 4)) * 2.0 ** -20 * size
        k = 1.0 if o[r] == 0 else 2.0 ** -30
        for h in range(0, 128, 16):
            u[r, h, h, 0] = k
            u[r, h + 8:h + 10, h] = k
    w = layers(rng)
    w[:, :, :10] = 0
    w[:, :, :, :, :, :10] = 0
    return {"x": x.reshape(N, 128, 4 * C).astype(BF), "u": u.reshape(N, 128, 512), "v": d["v"], **weights(rng, w), **ways(e, walks(rng))}
def setup_inputs_huge(rng):
    d = numbers_of(rng)
    c = np.stack([np.where(rng.permutation(C) % 2 == 0, -1.0, 0.25) for r in range(N)])
    c[rng.permutation(N) < N // 2] = -1
    x = 2.0 ** 30 * (0.8 + 0.2 * rng.random((N, 128, C, 4))) * c[:, None, :, None]
    s = np.stack([rng.permutation(8) % 2 * 2.0 - 1.0 for r in range(N)])
    a = 2.0 ** 30 * (1 - 0.1 * rng.random((N, 8, 16, 4))) * s[:, :, None, None]
    u = d["u"].reshape(N, 8, 16, 128, 4)
    for g in range(8): u[:, g, :, 16 * g] = a[:, g].astype(np.float32).astype(BF)
    w = np.zeros((N, 128, 4, 128, 4), np.float32)
    i = np.arange(128)
    for b in range(4): w[:, i, b, i, b] = -4
    return {"x": x.astype(np.float32).reshape(N, 128, 4 * C).astype(BF), "u": u.reshape(N, 128, 512), "v": d["v"], **weights(rng, w.astype(BF)), **ways(routes(rng), walks(rng))}
def setup_inputs_routes(rng):
    d = numbers_of(rng)
    x, u = d["x"].reshape(N, 8, 16, C, 4), d["u"].astype(np.float32).reshape(N, 8, 16, 128, 4)
    e, w = routes(rng), walks(rng)
    n = np.arange(C)
    for r in range(N):
        for g, k in enumerate(rng.permutation(8)):
            p = rng.permutation(C)
            if k == 0: e[r, g], w[r, g] = np.concatenate([p, p]), n
            if k == 1: e[r, g], w[r, g] = np.repeat(p, 2), (n + 1) % C
            if k == 2: e[r, g], w[r, g] = np.concatenate([p, p[::-1]]), (n - 1) % C
            if k == 3: e[r, g], w[r, g] = np.tile(p.reshape(L, S // 2), 2).reshape(-1), p[0]
            if k == 4:
                a = np.zeros((L, S), int)
                a[:, 0] = np.tile(p[:L // 2], 2)
                a[:, 1:] = rng.permutation(np.tile(p[L // 2:], 2)).reshape(L, S - 1)
                e[r, g], w[r, g] = a.reshape(-1), n ^ 1
            if k == 5:
                w[r, g] = e[r, g, 1]
                x[r, g, :, e[r, g, 0]] = (16 * np.sign(u[r, g, :, 16 * g])).astype(BF)
    return {"x": x.reshape(N, 128, 4 * C), "u": d["u"], "v": d["v"], **weights(rng, layers(rng)), **ways(e, w)}
def setup_inputs_spread(rng):
    d = setup_inputs(rng)
    d["x"] = big(wide(rng, N, 128, 4 * C, cols=6))
    return d
def check_inputs(d):
    b = []
    for k in ("x", "u", "v"):
        a = np.abs(d[k].astype(np.float32))
        if not (np.isfinite(a).all() and ((a == 0) | (a >= 2.0 ** -30) & (a <= 2.0 ** 30)).all()): b.append("a value of " + k)
    a = d["u"].astype(np.float32).reshape(N, 8, 16, 128, 4)
    for g in range(8):
        if (np.delete(a[:, :, :, 16 * g], g, axis=1) != 0).any(): b.append("u: a column that scores a group isn't zero outside it")
    none, least, most = [emit(mx_ref.quantize(np.full((128, 16), k, np.float32).astype(BF)))[1][0, 0] for k in (0.0, 2.0 ** -30, 2.0 ** 30)]
    for r in range(N):
        if ((d["wc"][r] == 0x7F) | (d["wc"][r] == 0xFF)).any(): b.append("wc: a code that is no number")
        s = mx_ref.live(d["ws"][r])
        if ((s != none) & ((s < least) | (s > most))).any(): b.append("ws: a scale out of range")
        if (np.sort(gentries(d["rt"][r]), axis=1) != np.arange(2 * C) // 2).any(): b.append("rt: a stop that isn't there exactly twice")
    if ((d["ft"] < 0) | (d["ft"] >= C)).any(): b.append("ft: a number that is no stop")
    return b
def reference(x, u, v, wc, ws, rt, ft):
    qu = [mx_ref.quantize(u[r]) for r in range(N)]
    lay = [pk(wc[r], ws[r]) for r in range(N)]
    way = [gentries(rt[r]) for r in range(N)]
    foot = [gentries(ft[r]) for r in range(N)]
    at = [np.argsort(way[r], axis=1, kind="stable").reshape(8, C, 2) for r in range(N)]
    now = [x[r] for r in range(N)]
    last = [None] * N
    for t in range(R):
        own, score, sent = [], [], []
        for r in range(N):
            q = mx_ref.quantize(now[r])
            s = mx_ref.matmul(qu[r], q)[::16] + np.float32(0.0)
            z = s[G, way[r]].reshape(8, L, S)
            e = np.take_along_axis(way[r].reshape(8, L, S), np.argmax(z, axis=2)[:, :, None], axis=2)[:, :, 0]
            own.append(decode(q))
            score.append(z)
            sent.append(mx_ref.quantize(gcols(now[r], e)))
        for r in range(N):
            guests = sent[(r - 1 - t) % N]
            z = mx_ref.matmul(qu[r], guests)[::16] + np.float32(0.0)
            c = np.concatenate([z[:, :, None], score[r][:, :, :S - 1]], axis=2)
            src = np.concatenate([np.tile(C + np.arange(L), (8, 1))[:, :, None], way[r].reshape(8, L, S)[:, :, :S - 1]], axis=2)
            m = np.maximum.accumulate(c, axis=2)
            above = np.zeros((8, L, S), bool)
            above[:, :, 1:] = c[:, :, 1:] > m[:, :, :-1]
            k = np.maximum.accumulate(np.where(above, np.arange(S), 0), axis=2)
            a, val = np.take_along_axis(src, k, axis=2).reshape(8, -1), m.reshape(8, -1)
            p0, p1 = at[r][:, :, 0], at[r][:, :, 1]
            p = np.where(val[G, p1] > val[G, p0], p1, p0)
            a, val = a[G, p], val[G, p]
            a = a[G, np.where(val[G, foot[r]] > val, foot[r], np.arange(C))]
            both = np.concatenate([own[r], decode(guests)], axis=1).astype(BF)
            q = mx_ref.quantize(((own[r] + gcols(both, a).astype(np.float32)) * np.float32(0.5)).astype(BF))
            now[r] = tile([own[r][:, b::4] + np.maximum(mx_ref.matmul(pick(lay[r], np.arange(128 * b, 128 * b + 128)), q), np.float32(0.0)) * np.float32(0.03125) for b in range(4)])
            last[r] = a
    y, oa = np.zeros((N, 128, C), np.float32), np.zeros((N, 8, C), np.float32)
    oc, osc = np.zeros((N, 128, 4 * C), np.uint8), np.zeros((N, 16, C), np.uint8)
    for r in range(N):
        q = mx_ref.quantize(now[r])
        y[r] = mx_ref.matmul(mx_ref.quantize(v[r]), q)
        oa[r] = last[r]
        oc[r], osc[r] = emit(q)
    return {"y": y, "oa": oa, "oc": oc, "osc": osc}

@@ -1,0 +1,475 @@
+from concourse.bass import DstId, RemoteDMATransfer
+from concourse.mybir import dt, AluOpType, ActivationFunctionType
+
+F32, BF, I32, U16, CODE, U8 = "float32", "bfloat16", "int32", "uint16", "float8_e4m3fn_x4", "uint8"
+R = 3
+NX = 3
+NXH = (2, 3)
+CUT0 = [0, 128, 352, 512]
+CUT1 = [0, 192, 448, 704, 896, 1024]
+CUT2 = [0, 192, 448, 704, 896, 1024]
+PLAN = "y03 y02 y00 y01 y13 q0 y10 y11 y12 f q1 x03 x00 x01 x02 d0 x13 x10 x11 x12 d1".split()
+LOW = -1.0e29
+
+SCRATCH = {}
+
+
+def _buf(dtype, **k):
+    for n, w in k.items():
+        SCRATCH[n] = ("sbuf", [128, w], dtype)
+
+
+_buf(BF, X0=1024, X1=1024, UB=512, VBF=512, ONE=528, EU=528, EH=528, ET=512, YT=1024, TH=256, TL=256, IH=256, IL=256,
+     HIT=512, CNT=512, CAP=512, MSK=512, MT=512, SG=512, SEG16=512, SEG32=512, HL=512)
+_buf(F32, RTF=48, RTT=64, WAY=32, WAYI=32, DW=32, CV=16, C4=4, I16=16, IR=32, S2=512, Z1=512, ZT=512, VB=1024, OW=1024,
+     G1=1024, G2=1024, GT=1024, NA=32, UU=32, CAND=128, DS=128, MX=136, NA8=128, UA=128, SEG8=128, ZW=64,
+     HW=1152, HC=512, TP=1024, RL=1024, IG=64, INX=64, WN=96, TA=64, HI32=32, DST=32, VI=512,
+     VAL=512, SW=512, P1=512, PS=512, VK=64, IOT=288, OAR=256, YO=256, FA=16)
+_buf(I32, RT=48, FT=16, PI=1, CI=4, HII=32, FI=16, VKI=64, A1=64, A2=64)
+_buf(U16, RTU=32, OFF1=32, WOFF=2, SOFF=2, NOFF=16, FOFF=16, UOFF=8, EOFF=8, AOFF=16, DSTU=32, OOFF=64, GOFF=64)
+_buf(CODE, QU=128, QB=128, QV=128, WC=512, EC=1024, QY=256, TF=256)
+_buf(U8, QUS=128, QBS=128, QVS=128, WS=512, ES=1024, QYS=256, TFS=256)
+for _t in range(R):
+    _buf(CODE, **{"TG%d" % _t: 288, "QE%d" % _t: 128})
+    _buf(U8, **{"TS%d" % _t: 384, "QES%d" % _t: 128})
+for _b in range(4):
+    SCRATCH["PA%d" % _b] = ("psum", [128, 512], F32)
+    SCRATCH["PB%d" % _b] = ("psum", [128, 512], F32)
+
+NDMA = 20
+SEMAPHORES = ["cv", "cs", "ct", "cg", "sent"] + ["arr%d" % t for t in range(R)] + ["d%d" % k for k in range(NDMA)]
+
+
+def rank_program(g, core, T, topo):
+    rank = T.rank_of(core)
+    if rank is None:
+        return
+    N = len(T.cores)
+    A, ACT = AluOpType, ActivationFunctionType
+    queue = {"v": g.vector, "s": g.scalar, "t": g.tensor, "g": g, "y": g.sync}
+    count = {}
+    known = {q: {} for q in queue}
+    log = {}
+    ndma = [0]
+
+    def r(name, a=0, b=None, s=1):
+        return (name, a, SCRATCH[name][1][1] if b is None else b, s)
+
+    def ap(v):
+        return T[v[0]][:, v[1]:v[2]:v[3]] if v[3] != 1 else T[v[0]][:, v[1]:v[2]]
+
+    def wait(q, sem, val, kn):
+        if known[q].get(sem, 0) < val:
+            queue[q].wait_ge(T.sem[sem], val)
+            known[q][sem] = val
+        for s_, v_ in kn.items():
+            if known[q].get(s_, 0) < v_:
+                known[q][s_] = v_
+
+    def issue(q, fn, reads, writes, sem=None, inc=1):
+        acc = [(v, False) for v in reads] + [(v, True) for v in writes]
+        best = {}
+        sets = []
+        for v, w in acc:
+            ps = SCRATCH[v[0]][0] == "psum"
+            cols = None if ps else frozenset(range(v[1], v[2], v[3]))
+            sets.append((v[0], cols, w))
+            for (c2, w2, q2, s2, n2, kn) in log.get(v[0], []):
+                if ps:
+                    hit = w or w2 or q2 != q
+                else:
+                    hit = (w or w2) and not cols.isdisjoint(c2)
+                if hit and n2 >= best.get(s2, (0, None))[0]:
+                    best[s2] = (n2, kn)
+        for s2, (n2, kn) in best.items():
+            if not any(k2.get(s2, 0) >= n2 for s3, (n3, k2) in best.items() if s3 != s2):
+                wait(q, s2, n2, kn)
+        for s2, (n2, kn) in best.items():
+            wait(q, s2, n2, kn)
+        sem = sem or "c" + q
+        ins = fn()
+        count[sem] = count.get(sem, 0) + inc
+        if ins is not None:
+            ins.then_inc(T.sem[sem], inc)
+        kn = dict(known[q])
+        for name, cols, w in sets:
+            log.setdefault(name, []).append((cols, w, q, sem, count[sem], kn))
+
+    def sc(x):
+        return ap(x) if isinstance(x, tuple) else x
+
+    def tups(*x):
+        return [e for e in x if isinstance(e, tuple)]
+
+    def src(i, off):
+        return ap(i).indirect(ap(off)) if off else ap(i)
+
+    def copy(o, i, off=None):
+        issue("v", lambda: g.vector.tensor_copy(ap(o), src(i, off)), tups(i, off), [o])
+
+    def act(o, i, off=None, func=None, scale=1.0):
+        f = func or ACT.Copy
+        if scale == 1.0:
+            issue("s", lambda: g.scalar.activation(ap(o), src(i, off), f), tups(i, off), [o])
+        else:
+            issue("s", lambda: g.scalar.activation(ap(o), src(i, off), f, scale=scale), tups(i, off), [o])
+
+    def tt(o, a, b, op, off=None):
+        issue("v", lambda: g.vector.tensor_tensor(ap(o), src(a, off), ap(b), op), tups(a, b, off), [o])
+
+    def ts(o, a, s1, op0, s2=None, op1=None):
+        if op1 is None:
+            issue("v", lambda: g.vector.tensor_scalar(ap(o), ap(a), sc(s1), None, op0), tups(a, s1), [o])
+        else:
+            issue("v", lambda: g.vector.tensor_scalar(ap(o), ap(a), sc(s1), sc(s2), op0, op1), tups(a, s1, s2), [o])
+
+    def scan(o, d0, d1, init, op0, op1):
+        issue("v", lambda: g.vector.tensor_tensor_scan(ap(o), ap(d0), ap(d1), init, op0, op1), [d0, d1], [o])
+
+    def tr(o, i):
+        issue("v", lambda: g.vector.transpose(ap(o), ap(i)), [i], [o])
+
+    def mset(o, c):
+        issue("v", lambda: g.vector.memset(ap(o), c), [], [o])
+
+    def quant(c, s, i):
+        issue("v", lambda: g.vector.quantize_mx(ap(c), ap(s), ap(i)), [i], [c, s])
+
+    def mm(o, wc, ws, xc, xs):
+        issue("t", lambda: g.tensor.matmul_mx(ap(o), ap(wc), ap(ws), ap(xc), ap(xs), True, True), [wc, ws, xc, xs], [o])
+
+    def iota(o, pat, base=0, cm=0):
+        if SCRATCH[o[0]][2] == I32:
+            issue("g", lambda: g.iota(ap(o), pat, base, cm), [], [o])
+        else:
+            issue("g", lambda: g.iota(ap(o), pat, base, cm, allow_small_or_imprecise_dtypes=True), [], [o])
+
+    def pick(o, i, pat, op, base, cm):
+        issue("g", lambda: g.affine_select(ap(o), ap(i), pat, op, 0.0, base, cm), [i], [o])
+
+    def dma(q, o, i, reads, writes):
+        sem = "d%d" % ndma[0]
+        ndma[0] += 1
+        issue(q, lambda: queue[q].dma_start(o, i), reads, writes, sem=sem, inc=16)
+
+    def col(k):
+        return r("CV", k, k + 1)
+
+    def unit(b, half=False):
+        k = 128 * (b + 4 if half else b)
+        return r("EC", k, k + 128), r("ES", k, k + 128)
+
+    dma("y", ap(r("UB")), T.u[:], [], [r("UB")])
+    dma("s", ap(r("RT", 0, 32)), T.rt[:], [], [r("RT", 0, 32)])
+    dma("y", ap(r("X0")), T.x[:], [], [r("X0")])
+    dma("s", ap(r("RT", 32, 48)), T.rt[:, 0:16], [], [r("RT", 32, 48)])
+    dma("s", ap(r("FT")), T.ft[:], [], [r("FT")])
+
+    iota(r("PI"), [[0, 1]], 0, 1)
+    mset(r("ONE", 0, 128), 1.0)
+    mset(r("EU"), 0.0)
+    iota(r("I16"), [[32, 16]])
+    pick(r("EU", 3, 515, 4), r("ONE", 0, 128), [[-1, 128]], A.is_equal, 0, 1)
+    iota(r("IH"), [[1, 16], [0, 16]])
+    iota(r("C4"), [[1, 4]])
+    ts(r("CI", 0, 1), r("PI"), 15, A.bitwise_and)
+    ts(r("CI", 1, 2), r("PI"), 16, A.bitwise_and)
+    ts(r("CI", 2, 3), r("PI"), 1, A.bitwise_and)
+    ts(r("CI", 3, 4), r("PI"), 31, A.bitwise_and)
+    ts(r("UOFF", 0, 8, 2), r("I16", 0, 4), 16.0, A.add)
+    copy(r("CV", 0, 4), r("CI"))
+    copy(r("UOFF", 1, 8, 2), r("I16", 0, 4))
+    act(r("EH", 0, 516), r("EU", 0, 516), scale=0.5)
+    act(r("VB", 0, 512), r("EU", 0, 512))
+    act(r("VB", 512, 1024), r("EU", 0, 512))
+    ts(col(4), col(1), 16.0, A.mult)
+    ts(col(5), col(1), -16.0, A.mult, 256.0, A.add)
+    ts(r("WOFF", 0, 1), col(1), 3.0, A.mult, col(0), A.add)
+    ts(col(8), col(0), 32.0, A.add)
+    for b in range(4):
+        quant(*unit(b), r("EU", 3 - b, 515 - b))
+    ts(r("WOFF", 1, 2), col(1), -1.0, A.mult, col(8), A.add)
+    for b in range(NX):
+        quant(*unit(b, True), r("EH", 3 - b, 515 - b))
+    iota(r("SEG16"), [[0, 32], [64, 16]])
+    iota(r("IL"), [[0, 16], [1, 16]])
+    for h in range(2):
+        iota(r("VI", 256 * h, 256 * h + 256), [[16 * 1024 + 1, 16], [1024 + 64, 16]], h * (256 * 1024 + 32))
+
+    def dealt(win, off, G, out, cuts):
+        for a, b in zip(cuts[1:], cuts[2:]):
+            act(r(G, a, b), win, r(off, a // 16, b // 16))
+        copy(r(G, 0, cuts[1]), win, r(off, 0, cuts[1] // 16))
+        for a, b in zip(cuts, cuts[1:]):
+            tr(r(out, a, b), r(G, a, b))
+
+    def inverse():
+        scan(r("CNT"), r("HIT"), r("HIT"), 0.0, A.add, A.max)
+        act(r("CAP"), r("HIT"), scale=64.0)
+        ts(r("TL"), r("IL"), col(0), A.is_equal, float(2 ** 20), A.mult)
+        act(r("HL"), r("TL"), r("RTU"))
+        issue("s", lambda: g.scalar.activation(ap(r("ONE", 0, 512)), ap(r("EU", 0, 512)), ACT.Identity, bias=1.0, scale=0.0),
+              [r("EU", 0, 512)], [r("ONE", 0, 512)])
+        pick(r("SEG32"), r("ONE", 0, 512), [[0, 16], [1, 32]], A.not_equal, 0, 0)
+        ts(r("HII"), r("RT", 0, 32), 240, A.bitwise_and)
+        scan(r("MSK"), r("CNT"), r("CAP"), 0.0, A.max, A.min)
+        ts(r("FI"), r("FT"), 240, A.bitwise_and)
+        ts(col(9), col(2), 31.0, A.mult, col(0), A.add)
+        tr(r("MT"), r("MSK"))
+        ts(r("HI32"), r("HII"), 2.0, A.mult, -1.0, A.add)
+        ts(col(10), col(1), 33.0 / 16.0, A.mult, col(9), A.add)
+        scan(r("SG"), r("SEG16"), r("MT"), 0.0, A.min, A.max)
+        ts(r("SOFF", 0, 1), col(10), 0.0, A.add)
+        ts(r("SOFF", 1, 2), col(10), 16.0, A.add)
+        copy(r("WN", 0, 32), r("SG", 15, 512, 16))
+        act(r("WN", 64, 96), r("SG", 15, 512, 16))
+        tt(r("FA"), r("FI"), r("FT"), A.add)
+        ts(r("NOFF"), r("I16"), col(3), A.add)
+        tr(r("TA", 0, 32), r("WN", 0, 32))
+        tr(r("TA", 32, 64), r("WN", 0, 32))
+        ts(r("FOFF"), r("FA"), col(1), A.add)
+        mset(r("SEG8"), 0.0)
+        tr(r("WN", 32, 64), r("TA", 16, 48))
+        scan(r("VAL"), r("VI"), r("HL"), 0.0, A.max, A.min)
+        tt(r("DST"), r("WN"), r("HI32"), A.add, r("SOFF"))
+        ts(col(6), col(1), 2.0, A.mult)
+        ts(col(7), col(1), -2.0, A.mult, 32.0, A.add)
+        copy(r("DSTU"), r("DST"))
+        for h in range(2):
+            act(r("WAYI", h, 32, 2), r("WAY", 16 * h, 16 * h + 16))
+        mset(r("SEG8", 7, 128, 8), LOW)
+        mset(r("MX", 0, 1), LOW)
+        unpack_own()
+        issue("v", lambda: g.vector.tensor_copy(ap(r("SW")).indirect(ap(r("DSTU"))), ap(r("VAL"))),
+              [r("VAL"), r("DSTU")], [r("SW")])
+        own_rows()
+        scan(r("P1"), r("SEG32"), r("SW"), 0.0, A.mult, A.max)
+        scan(r("PS"), r("SEG32"), r("SW"), 0.0, A.mult, A.add)
+        for l in range(2):
+            act(r("ZT", 16 * l + 1, 512, 32), r("P1", 31, 512, 32))
+        for l in range(2):
+            ts(r("VB", 16 * l + 2, 1024, 32), r("IR"), col(0), A.add)
+        for l in range(2):
+            tt(r("ZT", 16 * l, 512, 32), r("PS", 31, 512, 32), r("P1", 31, 512, 32), A.subtract)
+        mset(r("INX", 3, 64, 4), 0.0)
+        tr(r("Z1"), r("ZT"))
+        act(r("G1", 0, 256), r("Z1"), r("NOFF"))
+        act(r("G1", 256, 512), r("Z1"), r("FOFF"))
+        tr(r("OW", 0, 512), r("VB", 0, 512))
+        tr(r("GT", 0, 256), r("G1", 0, 256))
+        tr(r("OW", 512, 768), r("VB", 512, 768))
+        tr(r("GT", 256, 512), r("G1", 256, 512))
+        for k in range(4):
+            for p in range(2):
+                act(r("VK", 2 * k + p, 64, 8), r("GT", 256 * (k // 2) + 16 * p + k % 2, 256 * (k // 2) + 256, 32))
+        tr(r("OW", 768, 1024), r("VB", 768, 1024))
+        quant(r("QV"), r("QVS"), r("VBF"))
+        copy(r("VKI"), r("VK"))
+        ts(r("A1"), r("VKI"), 1023, A.bitwise_and)
+        ts(r("A2"), r("VKI"), 14, A.arith_shift_right)
+        for p in range(2):
+            ts(r("OOFF", p, 64, 2), r("A1", p, 64, 2), 16.0 * p, A.add)
+        for p in range(2):
+            ts(r("GOFF", p, 64, 2), r("A2", p, 64, 2), col(6 + p), A.add)
+
+    def own_rows():
+        act(r("VB", 80, 1024, 32), r("VB", 64, 1024, 32))
+        for l in range(2):
+            tt(r("VB", 65 + 16 * l, 1024, 32), r("UU", 0, 30), r("WAYI", 2, 32), A.add)
+
+    def unpack_own():
+        for b in range(4):
+            act(r("HW", 288 * b, 288 * b + 256), r("PA%d" % b, 0, 256), scale=1.0 if b < NX else 0.5)
+
+    def scores(c, s, a, b, banks, eng, between=None):
+        mm(r(banks[0], 0, b - a), r("QU"), r("QUS"), r(c, a, b), r(s, a, b))
+        mm(r(banks[1], 0, b - a), r("QB"), r("QBS"), r(c, a, b), r(s, a, b))
+        if between:
+            between()
+        act(r("S2", a, b), r(banks[0], 0, b - a))
+        eng(r("S2", 256 + a, 256 + b), r(banks[1], 0, b - a))
+
+    def lists():
+        tr(r("RTT", 0, 32), r("RTF", 0, 32))
+        tr(r("RTT", 32, 64), r("RTF", 16, 48))
+        mset(r("VB", 0, 64, 16), LOW)
+        for p in range(2):
+            ts(r("OFF1", p, 32, 2), r("RTT", 16 * p, 16 * p + 16), col(4 + p), A.add)
+        copy(r("WAY"), r("RTT"), r("WOFF"))
+        ts(r("TH"), r("IH"), col(0), A.is_equal)
+
+    X = r("X0")
+    for t in range(R):
+        TG, TS = "TG%d" % t, "TS%d" % t
+        own = (r(TG, 0, 256), r(TS, 0, 256))
+        if t == 0:
+            quant(r("QU"), r("QUS"), r("UB"))
+            copy(r("RTF"), r("RT"))
+            copy(r("RTU"), r("RT", 0, 32))
+            issue("v", lambda: g.vector.tensor_copy(ap(r("QB")).bitcast(dt.uint32),
+                                                    ap(r("QU")).bitcast(dt.uint32).indirect(ap(r("UOFF")))),
+                  [r("QU"), r("UOFF")], [r("QB")])
+            act(r("QBS"), r("QUS"), r("UOFF"))
+            quant(own[0], own[1], X)
+            act(r("ET"), r("EU", 0, 512), scale=0.0)
+            scores(TG, TS, 0, 256, ("PB0", "PB1"), copy, lists)
+            tt(r("DW", 0, 31), r("WAY", 0, 31), r("WAY", 1, 32), A.subtract)
+            mset(r("NA", 0, 2), 0.0)
+            dma("y", ap(r("WC")).bitcast(dt.uint8), T.wc[:], [r("X0")], [r("WC")])
+            dma("y", ap(r("WS")), T.ws[:], [], [r("WS")])
+            dma("y", ap(r("VBF")), T.v[:], [], [r("VBF")])
+        else:
+            for b in range(4):
+                mm(r("PA%d" % b, 0, 256), *unit(b, b < NX), *own)
+        dealt(r("S2"), "OFF1", "Z1", "ZT", CUT0)
+        if t == 0:
+            act(r("C4"), r("C4"), scale=0.25)
+            act(r("HIT"), r("TH"), r("RTU"))
+            copy(r("DW", 15, 32, 16), r("WAY", 15, 32, 16))
+        for h in range(2):
+            z = r("ZT", 16 * h, 480, 32)
+            scan(r("VB", 64 + 32 * h, 1024, 64), z, z, LOW, A.max, A.max)
+        for h in range(2):
+            tt(r("NA", 2 + h, 32, 2), r("ZT", 32 + 16 * h, 512, 32), r("VB", 64 + 32 * h, 1024, 64), A.is_le)
+        for h in range(2):
+            scan(r("UU", h, 32, 2), r("NA", h, 32, 2), r("DW", 16 * h, 16 * h + 16), 0.0, A.mult, A.add)
+        for h in range(2):
+            ts(r("EOFF", h, 8, 2), r("C4"), r("UU", 30 + h, 31 + h), A.add, 4.0, A.mult)
+        for e in range(2):
+            act(r("ET", 2 + e, 128, 4), X, r("EOFF", 4 + 2 * e, 6 + 2 * e))
+            copy(r("ET", e, 128, 4), X, r("EOFF", 2 * e, 2 * e + 2))
+        QE, QES = r("QE%d" % t), r("QES%d" % t)
+        if t > 0:
+            own_rows()
+        quant(QE, QES, r("ET"))
+        dst = T.cores[(rank + 1 + t) % N]
+        rid, pid = topo.addr(dst)[:2]
+        far = min((topo.engines(core, c) for c in T.cores if c != core), key=len)
+        eng = [e for e in topo.engines(core, dst) if e in far]
+        half = len(eng) // 2
+        masks = [sum(1 << e for e in eng[:half]), sum(1 << e for e in eng[half:])]
+        arr = "arr%d" % t
+
+        def send():
+            to = [DstId(rid=rid, pnc=pid)]
+            g.remote_dma_fused([
+                RemoteDMATransfer(dst_ids=to, dma_engine_mask=masks[0], remote_sem=T.sem[arr],
+                                  src=ap(r(QE[0], 0, 32)).bitcast(dt.uint8), dst=ap(r(TG, 256, 288)).bitcast(dt.uint8)),
+                RemoteDMATransfer(dst_ids=to, dma_engine_mask=masks[1], remote_sem=T.sem[arr],
+                                  src=ap(QES), dst=ap(r(TS, 256, 384)))], local_sem=T.sem.sent)
+        issue("g", send, [QE, QES], [], sem="sent", inc=2 * half)
+        count[arr] = 2 * half
+        for nm, a, b in ((TG, 256, 288), (TS, 256, 384)):
+            log.setdefault(nm, []).append((frozenset(range(a, b)), True, "far", arr, 2 * half, {}))
+
+        if t == 0:
+            iota(r("IR"), [[0, 16], [16, 2]], 256)
+            for b in range(4):
+                mm(r("PA%d" % b, 0, 256), *unit(b, b < NX), *own)
+            inverse()
+            iota(r("IOT"), [[1, 288]])
+        else:
+            unpack_own()
+            tr(r("OW", 64), r("VB", 64))
+        dealt(r("OW"), "OOFF", "G1", "GT", CUT1)
+        if t == 0:
+            for l in range(2):
+                copy(r("IG", 32 * l, 32 * l + 32), r("GT", 16 * l + 2, 1024, 32))
+        for l in range(2):
+            copy(r("CAND", 64 * l + 1, 64 * l + 64, 2), r("GT", 16 * l, 1024, 32))
+        if t == 0:
+            for k in range(3):
+                copy(r("INX", k, 64, 4), r("IG", k + 1, 64, 4))
+        for l in range(2):
+            so = r("GT", 16 * l + 1, 1024, 32)
+            tt(r("DS", 64 * l, 64 * l + 64, 2), r("IG", 32 * l, 32 * l + 32), so, A.subtract)
+            tt(r("DS", 64 * l + 1, 64 * l + 64, 2), so, r("INX", 32 * l, 32 * l + 32), A.subtract)
+
+        gst = (r(TG, 160, 288), r(TS, 160, 288))
+        mm(r("PB0", 0, 128), r("QU"), r("QUS"), *gst)
+        mm(r("PB1", 0, 128), r("QB"), r("QBS"), *gst)
+        act(r("ZW", 0, 32), r("PB0", 96, 128))
+        act(r("ZW", 32, 64), r("PB1", 96, 128))
+        for b in range(4):
+            mm(r("PA%d" % b, 0, 288), *unit(b, b < NX), r(TG), r(TS, 0, 288))
+        dealt(r("ZW"), "GOFF", "G2", "GT", CUT2)
+        copy(r("CAND", 0, 64, 2), r("GT", 0, 1024, 32))
+        copy(r("CAND", 64, 128, 2), r("GT", 16, 1024, 32))
+        for b in range(4):
+            act(r("HW", 288 * b + 256, 288 * b + 288), r("PA%d" % b, 256, 288), scale=1.0 if b < NX else 0.5)
+        for h in range(2):
+            for b in range(NXH[h], 4):
+                act(r("HC", 256 * (b - 2) + 128 * h, 256 * (b - 2) + 128 * h + 128), r("PA%d" % b, 128 * h, 128 * h + 128),
+                    scale=1.0 if b < NX else 0.5)
+        for a in (0, 64):
+            scan(r("MX", a + 1, a + 65), r("CAND", a, a + 64), r("SEG8", a, a + 64), LOW, A.max, A.add)
+        for a in (0, 64):
+            tt(r("NA8", a, a + 64), r("CAND", a, a + 64), r("MX", a, a + 64), A.is_le)
+        for a in (0, 64):
+            scan(r("UA", a, a + 64), r("NA8", a, a + 64), r("DS", a, a + 64), 0.0, A.mult, A.add)
+        for l in range(2):
+            copy(r("AOFF", l, 16, 2), r("UA", 64 * l + 7, 64 * l + 64, 8))
+        X = r("X1")
+        nq, ns = ("TG%d" % (t + 1), "TS%d" % (t + 1)) if t < R - 1 else ("TF", "TFS")
+        order = (3, 0, 1, 2)
+
+        def y_part(h, b):
+            a = 128 * h
+            out = r("YT", 4 * a + b, 4 * a + 512, 4)
+            if b < NXH[h]:
+                tt(out, r("TP", 256 * b + a, 256 * b + a + 128), r("PA%d" % b, a, a + 128), A.add)
+            else:
+                tt(out, r("HW", 288 * b, 288 * b + 288), r("HC", 256 * (b - 2) + a, 256 * (b - 2) + a + 128), A.add,
+                   r("AOFF", 8 * h, 8 * h + 8))
+
+        def y_layer(h):
+            a = 128 * h
+            quant(r("QY", a, a + 128), r("QYS", a, a + 128), r("YT", 4 * a, 4 * a + 512))
+            for b in order:
+                mm(r("PB%d" % b, 0, 128), r("WC", 128 * b, 128 * b + 128), r("WS", 128 * b, 128 * b + 128),
+                   r("QY", a, a + 128), r("QYS", a, a + 128))
+                act(r("RL", 256 * b + a, 256 * b + a + 128), r("PB%d" % b, 0, 128), func=ACT.Relu, scale=0.03125)
+
+        def x_part(h, b):
+            a = 128 * h
+            tt(r("X1", 4 * a + b, 4 * a + 512, 4), r("RL", 256 * b + a, 256 * b + a + 128), r("PA%d" % b, a, a + 128), A.add)
+
+        def x_done(h):
+            a = 128 * h
+            quant(r(nq, a, a + 128), r(ns, a, a + 128), r("X1", 4 * a, 4 * a + 512))
+            if t < R - 1:
+                scores(nq, ns, a, a + 128, ("PB3", "PB0") if a == 0 else ("PB1", "PB2"), act if a == 0 else copy)
+            else:
+                bank = r("PB3" if a == 0 else "PB0", 0, 128)
+                mm(bank, r("QV"), r("QVS"), r(nq, a, a + 128), r(ns, a, a + 128))
+                if a == 0:
+                    act(r("YO", 0, 128), bank)
+                    dma("y", T.y[:, 0:128], ap(r("YO", 0, 128)), [r("YO", 0, 128)], [])
+                    act(r("OAR"), r("IOT"), r("AOFF"))
+                    dma("y", T.oa[:], T.OAR[0:128:16, :], [r("OAR")], [])
+                else:
+                    act(r("YO", 128, 256), bank)
+
+        for h in range(2):
+            for b in range(NXH[h]):
+                act(r("TP", 256 * b + 128 * h, 256 * b + 128 * h + 128), r("HW", 288 * b, 288 * b + 288),
+                    r("AOFF", 8 * h, 8 * h + 8))
+        for step in PLAN:
+            if step[0] == "y":
+                y_part(int(step[1]), int(step[2]))
+            elif step[0] == "q":
+                y_layer(int(step[1]))
+            elif step[0] == "f":
+                for b in range(NX):
+                    mm(r("PA%d" % b, 0, 256), *unit(b), *own)
+            elif step[0] == "x":
+                x_part(int(step[1]), int(step[2]))
+            else:
+                x_done(int(step[1]))
+
+    dma("y", T.oc[:], ap(r("TF")).bitcast(dt.uint8), [r("TF")], [])
+    dma("s", T.y[:, 128:256], ap(r("YO", 128, 256)), [r("YO", 128, 256)], [])
+    for k in range(4):
+        dma("y", T.osc[4 * k:4 * k + 4, :], T.TFS[32 * k:32 * k + 4, :], [r("TFS")], [])
+    for sem, n in count.items():
+        wait("y", sem, n, {})

@@ -5,9 +5,9 @@ F32, BF, I32, U16, CODE, U8 = "float32", "bfloat16", "int32", "uint16", "float8_
 R = 3
 NX = 3
 NXH = (2, 3)
-CUT0 = [0, 128, 352, 512]
-CUT1 = [0, 192, 448, 704, 896, 1024]
-CUT2 = [0, 192, 448, 704, 896, 1024]
+CUT0 = [0, 160, 384, 512]
+CUT1 = [0, 224, 480, 736, 928, 1024]
+CUT2 = [0, 224, 480, 736, 928, 1024]
 PLAN = "y03 y02 y00 y01 y13 q0 y10 y11 y12 f q1 x03 x00 x01 x02 d0 x13 x10 x11 x12 d1".split()
 LOW = -1.0e29
 
@@ -20,9 +20,9 @@ def _buf(dtype, **k):
 
 
 _buf(BF, X0=1024, X1=1024, UB=512, VBF=512, ONE=528, EU=528, EH=528, ET=512, YT=1024, TH=256, TL=256, IH=256, IL=256,
-     HIT=512, CNT=512, CAP=512, MSK=512, MT=512, SG=512, SEG16=512, SEG32=512, HL=512)
+     HIT=512, CNT=512, CAP=528, MT=512, SG=512, SEG16=512, SEG32=512, HL=512)
 _buf(F32, RTF=48, RTT=64, WAY=32, WAYI=32, DW=32, CV=16, C4=4, I16=16, IR=32, S2=512, Z1=512, ZT=512, VB=1024, OW=1024,
-     G1=1024, G2=1024, GT=1024, NA=32, UU=32, CAND=128, DS=128, MX=136, NA8=128, UA=128, SEG8=128, ZW=64,
+     G1=1024, G2=1024, GT=1024, NA=32, UU=32, CAND=128, DS=128, MX=136, NA8=128, UA=128, SEG8=128, ZW=64, ZC=64,
      HW=1152, HC=512, TP=1024, RL=1024, IG=64, INX=64, WN=96, TA=64, HI32=32, DST=32, VI=512,
      VAL=512, SW=512, P1=512, PS=512, VK=64, IOT=288, OAR=256, YO=256, FA=16)
 _buf(I32, RT=48, FT=16, PI=1, CI=4, HII=32, FI=16, VKI=64, A1=64, A2=64)
@@ -114,6 +114,9 @@ def rank_program(g, core, T, topo):
         else:
             issue("s", lambda: g.scalar.activation(ap(o), src(i, off), f, scale=scale), tups(i, off), [o])
 
+    def lin(o, i, scale, bias):
+        issue("s", lambda: g.scalar.activation(ap(o), ap(i), ACT.Identity, bias=sc(bias), scale=scale), tups(i, bias), [o])
+
     def tt(o, a, b, op, off=None):
         issue("v", lambda: g.vector.tensor_tensor(ap(o), src(a, off), ap(b), op), tups(a, b, off), [o])
 
@@ -182,6 +185,7 @@ def rank_program(g, core, T, topo):
     act(r("EH", 0, 516), r("EU", 0, 516), scale=0.5)
     act(r("VB", 0, 512), r("EU", 0, 512))
     act(r("VB", 512, 1024), r("EU", 0, 512))
+    act(r("CAP", 0, 1), r("EU", 0, 1))
     ts(col(4), col(1), 16.0, A.mult)
     ts(col(5), col(1), -16.0, A.mult, 256.0, A.add)
     ts(r("WOFF", 0, 1), col(1), 3.0, A.mult, col(0), A.add)
@@ -191,6 +195,7 @@ def rank_program(g, core, T, topo):
     ts(r("WOFF", 1, 2), col(1), -1.0, A.mult, col(8), A.add)
     for b in range(NX):
         quant(*unit(b, True), r("EH", 3 - b, 515 - b))
+    ts(r("TH"), r("IH"), col(0), A.is_equal, 65.0, A.mult)
     iota(r("SEG16"), [[0, 32], [64, 16]])
     iota(r("IL"), [[0, 16], [1, 16]])
     for h in range(2):
@@ -203,67 +208,71 @@ def rank_program(g, core, T, topo):
         for a, b in zip(cuts, cuts[1:]):
             tr(r(out, a, b), r(G, a, b))
 
-    def inverse():
-        scan(r("CNT"), r("HIT"), r("HIT"), 0.0, A.add, A.max)
-        act(r("CAP"), r("HIT"), scale=64.0)
-        ts(r("TL"), r("IL"), col(0), A.is_equal, float(2 ** 20), A.mult)
+    def inverse(guests):
+        scan(r("CNT"), r("CAP", 0, 512), r("HIT"), -64.0, A.add, A.add)
+        lin(col(9), col(2), 31.0, col(0))
         act(r("HL"), r("TL"), r("RTU"))
-        issue("s", lambda: g.scalar.activation(ap(r("ONE", 0, 512)), ap(r("EU", 0, 512)), ACT.Identity, bias=1.0, scale=0.0),
-              [r("EU", 0, 512)], [r("ONE", 0, 512)])
+        lin(col(10), col(1), 33.0 / 16.0, col(9))
+        lin(r("ONE", 0, 512), r("EU", 0, 512), 0.0, 1.0)
         pick(r("SEG32"), r("ONE", 0, 512), [[0, 16], [1, 32]], A.not_equal, 0, 0)
         ts(r("HII"), r("RT", 0, 32), 240, A.bitwise_and)
-        scan(r("MSK"), r("CNT"), r("CAP"), 0.0, A.max, A.min)
         ts(r("FI"), r("FT"), 240, A.bitwise_and)
-        ts(col(9), col(2), 31.0, A.mult, col(0), A.add)
-        tr(r("MT"), r("MSK"))
+        tr(r("MT"), r("CNT"))
         ts(r("HI32"), r("HII"), 2.0, A.mult, -1.0, A.add)
-        ts(col(10), col(1), 33.0 / 16.0, A.mult, col(9), A.add)
-        scan(r("SG"), r("SEG16"), r("MT"), 0.0, A.min, A.max)
-        ts(r("SOFF", 0, 1), col(10), 0.0, A.add)
-        ts(r("SOFF", 1, 2), col(10), 16.0, A.add)
-        copy(r("WN", 0, 32), r("SG", 15, 512, 16))
-        act(r("WN", 64, 96), r("SG", 15, 512, 16))
         tt(r("FA"), r("FI"), r("FT"), A.add)
+        scan(r("SG"), r("SEG16"), r("MT"), 0.0, A.min, A.max)
         ts(r("NOFF"), r("I16"), col(3), A.add)
+        ts(r("FOFF"), r("FA"), col(1), A.add)
+        copy(r("WN", 0, 32), r("SG", 15, 512, 16))
+        copy(r("WN", 64, 96), r("SG", 15, 512, 16))
+        ts(r("SOFF", 0, 1), col(10), 0.0, A.add)
         tr(r("TA", 0, 32), r("WN", 0, 32))
         tr(r("TA", 32, 64), r("WN", 0, 32))
-        ts(r("FOFF"), r("FA"), col(1), A.add)
-        mset(r("SEG8"), 0.0)
+        ts(r("SOFF", 1, 2), col(10), 16.0, A.add)
         tr(r("WN", 32, 64), r("TA", 16, 48))
         scan(r("VAL"), r("VI"), r("HL"), 0.0, A.max, A.min)
         tt(r("DST"), r("WN"), r("HI32"), A.add, r("SOFF"))
-        ts(col(6), col(1), 2.0, A.mult)
-        ts(col(7), col(1), -2.0, A.mult, 32.0, A.add)
-        copy(r("DSTU"), r("DST"))
         for h in range(2):
             act(r("WAYI", h, 32, 2), r("WAY", 16 * h, 16 * h + 16))
-        mset(r("SEG8", 7, 128, 8), LOW)
-        mset(r("MX", 0, 1), LOW)
+        quant(r("QV"), r("QVS"), r("VBF"))
+        copy(r("DSTU"), r("DST"))
+        own_rows()
         unpack_own()
+        lin(col(6), col(1), 2.0, 0.0)
+        lin(col(7), col(1), -2.0, 32.0)
+        lin(r("SEG8"), r("EU", 0, 128), 0.0, 0.0)
+        lin(r("MX", 0, 1), r("EU", 0, 1), 0.0, LOW)
+        lin(r("INX", 3, 64, 4), r("EU", 0, 16), 0.0, 0.0)
+        for l in range(2):
+            lin(r("VB", 16 * l + 2, 1024, 32), r("IR"), 1.0, col(0))
+        lin(r("SEG8", 7, 128, 8), r("EU", 0, 16), 0.0, LOW)
         issue("v", lambda: g.vector.tensor_copy(ap(r("SW")).indirect(ap(r("DSTU"))), ap(r("VAL"))),
               [r("VAL"), r("DSTU")], [r("SW")])
-        own_rows()
         scan(r("P1"), r("SEG32"), r("SW"), 0.0, A.mult, A.max)
-        scan(r("PS"), r("SEG32"), r("SW"), 0.0, A.mult, A.add)
         for l in range(2):
             act(r("ZT", 16 * l + 1, 512, 32), r("P1", 31, 512, 32))
-        for l in range(2):
-            ts(r("VB", 16 * l + 2, 1024, 32), r("IR"), col(0), A.add)
+        guests()
+        for h in range(2):
+            for p in range(2):
+                act(r("ZW", 32 * h + 16 * p, 32 * h + 16 * p + 16), r("PB%d" % p, 96 + 16 * h, 112 + 16 * h))
+        scan(r("PS"), r("SEG32"), r("SW"), 0.0, A.mult, A.add)
         for l in range(2):
             tt(r("ZT", 16 * l, 512, 32), r("PS", 31, 512, 32), r("P1", 31, 512, 32), A.subtract)
-        mset(r("INX", 3, 64, 4), 0.0)
+        tr(r("ZC"), r("ZW"))
+        for l in range(2):
+            for h in range(2):
+                lin(r("VB", 32 * h + 16 * l + 3, 1024, 64), r("I16"), 0.0, r("ZC", 32 * h, 32 * h + 1))
         tr(r("Z1"), r("ZT"))
         act(r("G1", 0, 256), r("Z1"), r("NOFF"))
         act(r("G1", 256, 512), r("Z1"), r("FOFF"))
-        tr(r("OW", 0, 512), r("VB", 0, 512))
+        tr(r("OW", 0, 576), r("VB", 0, 576))
         tr(r("GT", 0, 256), r("G1", 0, 256))
-        tr(r("OW", 512, 768), r("VB", 512, 768))
+        tr(r("OW", 576, 768), r("VB", 576, 768))
         tr(r("GT", 256, 512), r("G1", 256, 512))
         for k in range(4):
             for p in range(2):
                 act(r("VK", 2 * k + p, 64, 8), r("GT", 256 * (k // 2) + 16 * p + k % 2, 256 * (k // 2) + 256, 32))
         tr(r("OW", 768, 1024), r("VB", 768, 1024))
-        quant(r("QV"), r("QVS"), r("VBF"))
         copy(r("VKI"), r("VK"))
         ts(r("A1"), r("VKI"), 1023, A.bitwise_and)
         ts(r("A2"), r("VKI"), 14, A.arith_shift_right)
@@ -296,7 +305,7 @@ def rank_program(g, core, T, topo):
         for p in range(2):
             ts(r("OFF1", p, 32, 2), r("RTT", 16 * p, 16 * p + 16), col(4 + p), A.add)
         copy(r("WAY"), r("RTT"), r("WOFF"))
-        ts(r("TH"), r("IH"), col(0), A.is_equal)
+        mset(r("ET", 128, 512), 0.0)
 
     X = r("X0")
     for t in range(R):
@@ -310,8 +319,8 @@ def rank_program(g, core, T, topo):
                                                     ap(r("QU")).bitcast(dt.uint32).indirect(ap(r("UOFF")))),
                   [r("QU"), r("UOFF")], [r("QB")])
             act(r("QBS"), r("QUS"), r("UOFF"))
+            act(r("HIT", 0, 256), r("TH"), r("RTU", 0, 16))
             quant(own[0], own[1], X)
-            act(r("ET"), r("EU", 0, 512), scale=0.0)
             scores(TG, TS, 0, 256, ("PB0", "PB1"), copy, lists)
             tt(r("DW", 0, 31), r("WAY", 0, 31), r("WAY", 1, 32), A.subtract)
             mset(r("NA", 0, 2), 0.0)
@@ -324,7 +333,8 @@ def rank_program(g, core, T, topo):
         dealt(r("S2"), "OFF1", "Z1", "ZT", CUT0)
         if t == 0:
             act(r("C4"), r("C4"), scale=0.25)
-            act(r("HIT"), r("TH"), r("RTU"))
+            act(r("HIT", 256, 512), r("TH"), r("RTU", 16, 32))
+            act(r("CAP", 1, 513), r("HIT"), scale=-64.0 / 65.0)
             copy(r("DW", 15, 32, 16), r("WAY", 15, 32, 16))
         for h in range(2):
             z = r("ZT", 16 * h, 480, 32)
@@ -339,8 +349,8 @@ def rank_program(g, core, T, topo):
             act(r("ET", 2 + e, 128, 4), X, r("EOFF", 4 + 2 * e, 6 + 2 * e))
             copy(r("ET", e, 128, 4), X, r("EOFF", 2 * e, 2 * e + 2))
         QE, QES = r("QE%d" % t), r("QES%d" % t)
-        if t > 0:
-            own_rows()
+        if t == 0:
+            ts(r("TL"), r("IL"), col(0), A.is_equal, float(2 ** 20), A.mult)
         quant(QE, QES, r("ET"))
         dst = T.cores[(rank + 1 + t) % N]
         rid, pid = topo.addr(dst)[:2]
@@ -362,13 +372,21 @@ def rank_program(g, core, T, topo):
         for nm, a, b in ((TG, 256, 288), (TS, 256, 384)):
             log.setdefault(nm, []).append((frozenset(range(a, b)), True, "far", arr, 2 * half, {}))
 
+        def guests():
+            gst = (r(TG, 160, 288), r(TS, 160, 288))
+            mm(r("PB0", 0, 128), r("QU"), r("QUS"), *gst)
+            mm(r("PB1", 0, 128), r("QB"), r("QBS"), *gst)
+            for b in range(4):
+                mm(r("PA%d" % b, 0, 288), *unit(b, b < NX), r(TG), r(TS, 0, 288))
+
         if t == 0:
             iota(r("IR"), [[0, 16], [16, 2]], 256)
             for b in range(4):
                 mm(r("PA%d" % b, 0, 256), *unit(b, b < NX), *own)
-            inverse()
+            inverse(guests)
             iota(r("IOT"), [[1, 288]])
         else:
+            own_rows()
             unpack_own()
             tr(r("OW", 64), r("VB", 64))
         dealt(r("OW"), "OOFF", "G1", "GT", CUT1)
@@ -376,7 +394,9 @@ def rank_program(g, core, T, topo):
             for l in range(2):
                 copy(r("IG", 32 * l, 32 * l + 32), r("GT", 16 * l + 2, 1024, 32))
         for l in range(2):
-            copy(r("CAND", 64 * l + 1, 64 * l + 64, 2), r("GT", 16 * l, 1024, 32))
+            (act if t == 0 else copy)(r("CAND", 64 * l + 1, 64 * l + 64, 2), r("GT", 16 * l, 1024, 32))
+            if t == 0:
+                act(r("CAND", 64 * l, 64 * l + 64, 2), r("GT", 16 * l + 3, 1024, 32))
         if t == 0:
             for k in range(3):
                 copy(r("INX", k, 64, 4), r("IG", k + 1, 64, 4))
@@ -385,16 +405,13 @@ def rank_program(g, core, T, topo):
             tt(r("DS", 64 * l, 64 * l + 64, 2), r("IG", 32 * l, 32 * l + 32), so, A.subtract)
             tt(r("DS", 64 * l + 1, 64 * l + 64, 2), so, r("INX", 32 * l, 32 * l + 32), A.subtract)
 
-        gst = (r(TG, 160, 288), r(TS, 160, 288))
-        mm(r("PB0", 0, 128), r("QU"), r("QUS"), *gst)
-        mm(r("PB1", 0, 128), r("QB"), r("QBS"), *gst)
-        act(r("ZW", 0, 32), r("PB0", 96, 128))
-        act(r("ZW", 32, 64), r("PB1", 96, 128))
-        for b in range(4):
-            mm(r("PA%d" % b, 0, 288), *unit(b, b < NX), r(TG), r(TS, 0, 288))
-        dealt(r("ZW"), "GOFF", "G2", "GT", CUT2)
-        copy(r("CAND", 0, 64, 2), r("GT", 0, 1024, 32))
-        copy(r("CAND", 64, 128, 2), r("GT", 16, 1024, 32))
+        if t > 0:
+            guests()
+            act(r("ZW", 0, 32), r("PB0", 96, 128))
+            act(r("ZW", 32, 64), r("PB1", 96, 128))
+            dealt(r("ZW"), "GOFF", "G2", "GT", CUT2)
+            for l in range(2):
+                copy(r("CAND", 64 * l, 64 * l + 64, 2), r("GT", 16 * l, 1024, 32))
         for b in range(4):
             act(r("HW", 288 * b + 256, 288 * b + 288), r("PA%d" % b, 256, 288), scale=1.0 if b < NX else 0.5)
         for h in range(2):

from concourse.bass import DstId, RemoteDMATransfer
from concourse.mybir import dt, AluOpType, ActivationFunctionType

F32, BF, I32, U16, CODE, U8 = "float32", "bfloat16", "int32", "uint16", "float8_e4m3fn_x4", "uint8"
R = 3
NX = 3
NXH = (2, 3)
CUT0 = [0, 160, 384, 512]
CUT1 = [0, 224, 480, 736, 928, 1024]
CUT2 = [0, 224, 480, 736, 928, 1024]
PLAN = "y03 y02 y00 y01 y13 q0 y10 y11 y12 f q1 x03 x00 x01 x02 d0 x13 x10 x11 x12 d1".split()
LOW = -1.0e29

SCRATCH = {}


def _buf(dtype, **k):
    for n, w in k.items():
        SCRATCH[n] = ("sbuf", [128, w], dtype)


_buf(BF, X0=1024, X1=1024, UB=512, VBF=512, ONE=528, EU=528, EH=528, ET=512, YT=1024, TH=256, TL=256, IH=256, IL=256,
     HIT=512, CNT=512, CAP=528, MT=512, SG=512, SEG16=512, SEG32=512, HL=512)
_buf(F32, RTF=48, RTT=64, WAY=32, WAYI=32, DW=32, CV=16, C4=4, I16=16, IR=32, S2=512, Z1=512, ZT=512, VB=1024, OW=1024,
     G1=1024, G2=1024, GT=1024, NA=32, UU=32, CAND=128, DS=128, MX=136, NA8=128, UA=128, SEG8=128, ZW=64, ZC=64,
     HW=1152, HC=512, TP=1024, RL=1024, IG=64, INX=64, WN=96, TA=64, HI32=32, DST=32, VI=512,
     VAL=512, SW=512, P1=512, PS=512, VK=64, IOT=288, OAR=256, YO=256, FA=16)
_buf(I32, RT=48, FT=16, PI=1, CI=4, HII=32, FI=16, VKI=64, A1=64, A2=64)
_buf(U16, RTU=32, OFF1=32, WOFF=2, SOFF=2, NOFF=16, FOFF=16, UOFF=8, EOFF=8, AOFF=16, DSTU=32, OOFF=64, GOFF=64)
_buf(CODE, QU=128, QB=128, QV=128, WC=512, EC=1024, QY=256, TF=256)
_buf(U8, QUS=128, QBS=128, QVS=128, WS=512, ES=1024, QYS=256, TFS=256)
for _t in range(R):
    _buf(CODE, **{"TG%d" % _t: 288, "QE%d" % _t: 128})
    _buf(U8, **{"TS%d" % _t: 384, "QES%d" % _t: 128})
for _b in range(4):
    SCRATCH["PA%d" % _b] = ("psum", [128, 512], F32)
    SCRATCH["PB%d" % _b] = ("psum", [128, 512], F32)

NDMA = 20
SEMAPHORES = ["cv", "cs", "ct", "cg", "sent"] + ["arr%d" % t for t in range(R)] + ["d%d" % k for k in range(NDMA)]


def rank_program(g, core, T, topo):
    rank = T.rank_of(core)
    if rank is None:
        return
    N = len(T.cores)
    A, ACT = AluOpType, ActivationFunctionType
    queue = {"v": g.vector, "s": g.scalar, "t": g.tensor, "g": g, "y": g.sync}
    count = {}
    known = {q: {} for q in queue}
    log = {}
    ndma = [0]

    def r(name, a=0, b=None, s=1):
        return (name, a, SCRATCH[name][1][1] if b is None else b, s)

    def ap(v):
        return T[v[0]][:, v[1]:v[2]:v[3]] if v[3] != 1 else T[v[0]][:, v[1]:v[2]]

    def wait(q, sem, val, kn):
        if known[q].get(sem, 0) < val:
            queue[q].wait_ge(T.sem[sem], val)
            known[q][sem] = val
        for s_, v_ in kn.items():
            if known[q].get(s_, 0) < v_:
                known[q][s_] = v_

    def issue(q, fn, reads, writes, sem=None, inc=1):
        acc = [(v, False) for v in reads] + [(v, True) for v in writes]
        best = {}
        sets = []
        for v, w in acc:
            ps = SCRATCH[v[0]][0] == "psum"
            cols = None if ps else frozenset(range(v[1], v[2], v[3]))
            sets.append((v[0], cols, w))
            for (c2, w2, q2, s2, n2, kn) in log.get(v[0], []):
                if ps:
                    hit = w or w2 or q2 != q
                else:
                    hit = (w or w2) and not cols.isdisjoint(c2)
                if hit and n2 >= best.get(s2, (0, None))[0]:
                    best[s2] = (n2, kn)
        for s2, (n2, kn) in best.items():
            if not any(k2.get(s2, 0) >= n2 for s3, (n3, k2) in best.items() if s3 != s2):
                wait(q, s2, n2, kn)
        for s2, (n2, kn) in best.items():
            wait(q, s2, n2, kn)
        sem = sem or "c" + q
        ins = fn()
        count[sem] = count.get(sem, 0) + inc
        if ins is not None:
            ins.then_inc(T.sem[sem], inc)
        kn = dict(known[q])
        for name, cols, w in sets:
            log.setdefault(name, []).append((cols, w, q, sem, count[sem], kn))

    def sc(x):
        return ap(x) if isinstance(x, tuple) else x

    def tups(*x):
        return [e for e in x if isinstance(e, tuple)]

    def src(i, off):
        return ap(i).indirect(ap(off)) if off else ap(i)

    def copy(o, i, off=None):
        issue("v", lambda: g.vector.tensor_copy(ap(o), src(i, off)), tups(i, off), [o])

    def act(o, i, off=None, func=None, scale=1.0):
        f = func or ACT.Copy
        if scale == 1.0:
            issue("s", lambda: g.scalar.activation(ap(o), src(i, off), f), tups(i, off), [o])
        else:
            issue("s", lambda: g.scalar.activation(ap(o), src(i, off), f, scale=scale), tups(i, off), [o])

    def lin(o, i, scale, bias):
        issue("s", lambda: g.scalar.activation(ap(o), ap(i), ACT.Identity, bias=sc(bias), scale=scale), tups(i, bias), [o])

    def tt(o, a, b, op, off=None):
        issue("v", lambda: g.vector.tensor_tensor(ap(o), src(a, off), ap(b), op), tups(a, b, off), [o])

    def ts(o, a, s1, op0, s2=None, op1=None):
        if op1 is None:
            issue("v", lambda: g.vector.tensor_scalar(ap(o), ap(a), sc(s1), None, op0), tups(a, s1), [o])
        else:
            issue("v", lambda: g.vector.tensor_scalar(ap(o), ap(a), sc(s1), sc(s2), op0, op1), tups(a, s1, s2), [o])

    def scan(o, d0, d1, init, op0, op1):
        issue("v", lambda: g.vector.tensor_tensor_scan(ap(o), ap(d0), ap(d1), init, op0, op1), [d0, d1], [o])

    def tr(o, i):
        issue("v", lambda: g.vector.transpose(ap(o), ap(i)), [i], [o])

    def mset(o, c):
        issue("v", lambda: g.vector.memset(ap(o), c), [], [o])

    def quant(c, s, i):
        issue("v", lambda: g.vector.quantize_mx(ap(c), ap(s), ap(i)), [i], [c, s])

    def mm(o, wc, ws, xc, xs):
        issue("t", lambda: g.tensor.matmul_mx(ap(o), ap(wc), ap(ws), ap(xc), ap(xs), True, True), [wc, ws, xc, xs], [o])

    def iota(o, pat, base=0, cm=0):
        if SCRATCH[o[0]][2] == I32:
            issue("g", lambda: g.iota(ap(o), pat, base, cm), [], [o])
        else:
            issue("g", lambda: g.iota(ap(o), pat, base, cm, allow_small_or_imprecise_dtypes=True), [], [o])

    def pick(o, i, pat, op, base, cm):
        issue("g", lambda: g.affine_select(ap(o), ap(i), pat, op, 0.0, base, cm), [i], [o])

    def dma(q, o, i, reads, writes):
        sem = "d%d" % ndma[0]
        ndma[0] += 1
        issue(q, lambda: queue[q].dma_start(o, i), reads, writes, sem=sem, inc=16)

    def col(k):
        return r("CV", k, k + 1)

    def unit(b, half=False):
        k = 128 * (b + 4 if half else b)
        return r("EC", k, k + 128), r("ES", k, k + 128)

    dma("y", ap(r("UB")), T.u[:], [], [r("UB")])
    dma("s", ap(r("RT", 0, 32)), T.rt[:], [], [r("RT", 0, 32)])
    dma("y", ap(r("X0")), T.x[:], [], [r("X0")])
    dma("s", ap(r("RT", 32, 48)), T.rt[:, 0:16], [], [r("RT", 32, 48)])
    dma("s", ap(r("FT")), T.ft[:], [], [r("FT")])

    iota(r("PI"), [[0, 1]], 0, 1)
    mset(r("ONE", 0, 128), 1.0)
    mset(r("EU"), 0.0)
    iota(r("I16"), [[32, 16]])
    pick(r("EU", 3, 515, 4), r("ONE", 0, 128), [[-1, 128]], A.is_equal, 0, 1)
    iota(r("IH"), [[1, 16], [0, 16]])
    iota(r("C4"), [[1, 4]])
    ts(r("CI", 0, 1), r("PI"), 15, A.bitwise_and)
    ts(r("CI", 1, 2), r("PI"), 16, A.bitwise_and)
    ts(r("CI", 2, 3), r("PI"), 1, A.bitwise_and)
    ts(r("CI", 3, 4), r("PI"), 31, A.bitwise_and)
    ts(r("UOFF", 0, 8, 2), r("I16", 0, 4), 16.0, A.add)
    copy(r("CV", 0, 4), r("CI"))
    copy(r("UOFF", 1, 8, 2), r("I16", 0, 4))
    act(r("EH", 0, 516), r("EU", 0, 516), scale=0.5)
    act(r("VB", 0, 512), r("EU", 0, 512))
    act(r("VB", 512, 1024), r("EU", 0, 512))
    act(r("CAP", 0, 1), r("EU", 0, 1))
    ts(col(4), col(1), 16.0, A.mult)
    ts(col(5), col(1), -16.0, A.mult, 256.0, A.add)
    ts(r("WOFF", 0, 1), col(1), 3.0, A.mult, col(0), A.add)
    ts(col(8), col(0), 32.0, A.add)
    for b in range(4):
        quant(*unit(b), r("EU", 3 - b, 515 - b))
    ts(r("WOFF", 1, 2), col(1), -1.0, A.mult, col(8), A.add)
    for b in range(NX):
        quant(*unit(b, True), r("EH", 3 - b, 515 - b))
    ts(r("TH"), r("IH"), col(0), A.is_equal, 65.0, A.mult)
    iota(r("SEG16"), [[0, 32], [64, 16]])
    iota(r("IL"), [[0, 16], [1, 16]])
    for h in range(2):
        iota(r("VI", 256 * h, 256 * h + 256), [[16 * 1024 + 1, 16], [1024 + 64, 16]], h * (256 * 1024 + 32))

    def dealt(win, off, G, out, cuts):
        for a, b in zip(cuts[1:], cuts[2:]):
            act(r(G, a, b), win, r(off, a // 16, b // 16))
        copy(r(G, 0, cuts[1]), win, r(off, 0, cuts[1] // 16))
        for a, b in zip(cuts, cuts[1:]):
            tr(r(out, a, b), r(G, a, b))

    def inverse(guests):
        scan(r("CNT"), r("CAP", 0, 512), r("HIT"), -64.0, A.add, A.add)
        lin(col(9), col(2), 31.0, col(0))
        act(r("HL"), r("TL"), r("RTU"))
        lin(col(10), col(1), 33.0 / 16.0, col(9))
        lin(r("ONE", 0, 512), r("EU", 0, 512), 0.0, 1.0)
        pick(r("SEG32"), r("ONE", 0, 512), [[0, 16], [1, 32]], A.not_equal, 0, 0)
        ts(r("HII"), r("RT", 0, 32), 240, A.bitwise_and)
        ts(r("FI"), r("FT"), 240, A.bitwise_and)
        tr(r("MT"), r("CNT"))
        ts(r("HI32"), r("HII"), 2.0, A.mult, -1.0, A.add)
        tt(r("FA"), r("FI"), r("FT"), A.add)
        scan(r("SG"), r("SEG16"), r("MT"), 0.0, A.min, A.max)
        ts(r("NOFF"), r("I16"), col(3), A.add)
        ts(r("FOFF"), r("FA"), col(1), A.add)
        copy(r("WN", 0, 32), r("SG", 15, 512, 16))
        copy(r("WN", 64, 96), r("SG", 15, 512, 16))
        ts(r("SOFF", 0, 1), col(10), 0.0, A.add)
        tr(r("TA", 0, 32), r("WN", 0, 32))
        tr(r("TA", 32, 64), r("WN", 0, 32))
        ts(r("SOFF", 1, 2), col(10), 16.0, A.add)
        tr(r("WN", 32, 64), r("TA", 16, 48))
        scan(r("VAL"), r("VI"), r("HL"), 0.0, A.max, A.min)
        tt(r("DST"), r("WN"), r("HI32"), A.add, r("SOFF"))
        for h in range(2):
            act(r("WAYI", h, 32, 2), r("WAY", 16 * h, 16 * h + 16))
        quant(r("QV"), r("QVS"), r("VBF"))
        copy(r("DSTU"), r("DST"))
        own_rows()
        unpack_own()
        lin(col(6), col(1), 2.0, 0.0)
        lin(col(7), col(1), -2.0, 32.0)
        lin(r("SEG8"), r("EU", 0, 128), 0.0, 0.0)
        lin(r("MX", 0, 1), r("EU", 0, 1), 0.0, LOW)
        lin(r("INX", 3, 64, 4), r("EU", 0, 16), 0.0, 0.0)
        for l in range(2):
            lin(r("VB", 16 * l + 2, 1024, 32), r("IR"), 1.0, col(0))
        lin(r("SEG8", 7, 128, 8), r("EU", 0, 16), 0.0, LOW)
        issue("v", lambda: g.vector.tensor_copy(ap(r("SW")).indirect(ap(r("DSTU"))), ap(r("VAL"))),
              [r("VAL"), r("DSTU")], [r("SW")])
        scan(r("P1"), r("SEG32"), r("SW"), 0.0, A.mult, A.max)
        for l in range(2):
            act(r("ZT", 16 * l + 1, 512, 32), r("P1", 31, 512, 32))
        guests()
        for h in range(2):
            for p in range(2):
                act(r("ZW", 32 * h + 16 * p, 32 * h + 16 * p + 16), r("PB%d" % p, 96 + 16 * h, 112 + 16 * h))
        scan(r("PS"), r("SEG32"), r("SW"), 0.0, A.mult, A.add)
        for l in range(2):
            tt(r("ZT", 16 * l, 512, 32), r("PS", 31, 512, 32), r("P1", 31, 512, 32), A.subtract)
        tr(r("ZC"), r("ZW"))
        for l in range(2):
            for h in range(2):
                lin(r("VB", 32 * h + 16 * l + 3, 1024, 64), r("I16"), 0.0, r("ZC", 32 * h, 32 * h + 1))
        tr(r("Z1"), r("ZT"))
        act(r("G1", 0, 256), r("Z1"), r("NOFF"))
        act(r("G1", 256, 512), r("Z1"), r("FOFF"))
        tr(r("OW", 0, 576), r("VB", 0, 576))
        tr(r("GT", 0, 256), r("G1", 0, 256))
        tr(r("OW", 576, 768), r("VB", 576, 768))
        tr(r("GT", 256, 512), r("G1", 256, 512))
        for k in range(4):
            for p in range(2):
                act(r("VK", 2 * k + p, 64, 8), r("GT", 256 * (k // 2) + 16 * p + k % 2, 256 * (k // 2) + 256, 32))
        tr(r("OW", 768, 1024), r("VB", 768, 1024))
        copy(r("VKI"), r("VK"))
        ts(r("A1"), r("VKI"), 1023, A.bitwise_and)
        ts(r("A2"), r("VKI"), 14, A.arith_shift_right)
        for p in range(2):
            ts(r("OOFF", p, 64, 2), r("A1", p, 64, 2), 16.0 * p, A.add)
        for p in range(2):
            ts(r("GOFF", p, 64, 2), r("A2", p, 64, 2), col(6 + p), A.add)

    def own_rows():
        act(r("VB", 80, 1024, 32), r("VB", 64, 1024, 32))
        for l in range(2):
            tt(r("VB", 65 + 16 * l, 1024, 32), r("UU", 0, 30), r("WAYI", 2, 32), A.add)

    def unpack_own():
        for b in range(4):
            act(r("HW", 288 * b, 288 * b + 256), r("PA%d" % b, 0, 256), scale=1.0 if b < NX else 0.5)

    def scores(c, s, a, b, banks, eng, between=None):
        mm(r(banks[0], 0, b - a), r("QU"), r("QUS"), r(c, a, b), r(s, a, b))
        mm(r(banks[1], 0, b - a), r("QB"), r("QBS"), r(c, a, b), r(s, a, b))
        if between:
            between()
        act(r("S2", a, b), r(banks[0], 0, b - a))
        eng(r("S2", 256 + a, 256 + b), r(banks[1], 0, b - a))

    def lists():
        tr(r("RTT", 0, 32), r("RTF", 0, 32))
        tr(r("RTT", 32, 64), r("RTF", 16, 48))
        mset(r("VB", 0, 64, 16), LOW)
        for p in range(2):
            ts(r("OFF1", p, 32, 2), r("RTT", 16 * p, 16 * p + 16), col(4 + p), A.add)
        copy(r("WAY"), r("RTT"), r("WOFF"))
        mset(r("ET", 128, 512), 0.0)

    X = r("X0")
    for t in range(R):
        TG, TS = "TG%d" % t, "TS%d" % t
        own = (r(TG, 0, 256), r(TS, 0, 256))
        if t == 0:
            quant(r("QU"), r("QUS"), r("UB"))
            copy(r("RTF"), r("RT"))
            copy(r("RTU"), r("RT", 0, 32))
            issue("v", lambda: g.vector.tensor_copy(ap(r("QB")).bitcast(dt.uint32),
                                                    ap(r("QU")).bitcast(dt.uint32).indirect(ap(r("UOFF")))),
                  [r("QU"), r("UOFF")], [r("QB")])
            act(r("QBS"), r("QUS"), r("UOFF"))
            act(r("HIT", 0, 256), r("TH"), r("RTU", 0, 16))
            quant(own[0], own[1], X)
            scores(TG, TS, 0, 256, ("PB0", "PB1"), copy, lists)
            tt(r("DW", 0, 31), r("WAY", 0, 31), r("WAY", 1, 32), A.subtract)
            mset(r("NA", 0, 2), 0.0)
            dma("y", ap(r("WC")).bitcast(dt.uint8), T.wc[:], [r("X0")], [r("WC")])
            dma("y", ap(r("WS")), T.ws[:], [], [r("WS")])
            dma("y", ap(r("VBF")), T.v[:], [], [r("VBF")])
        else:
            for b in range(4):
                mm(r("PA%d" % b, 0, 256), *unit(b, b < NX), *own)
        dealt(r("S2"), "OFF1", "Z1", "ZT", CUT0)
        if t == 0:
            act(r("C4"), r("C4"), scale=0.25)
            act(r("HIT", 256, 512), r("TH"), r("RTU", 16, 32))
            act(r("CAP", 1, 513), r("HIT"), scale=-64.0 / 65.0)
            copy(r("DW", 15, 32, 16), r("WAY", 15, 32, 16))
        for h in range(2):
            z = r("ZT", 16 * h, 480, 32)
            scan(r("VB", 64 + 32 * h, 1024, 64), z, z, LOW, A.max, A.max)
        for h in range(2):
            tt(r("NA", 2 + h, 32, 2), r("ZT", 32 + 16 * h, 512, 32), r("VB", 64 + 32 * h, 1024, 64), A.is_le)
        for h in range(2):
            scan(r("UU", h, 32, 2), r("NA", h, 32, 2), r("DW", 16 * h, 16 * h + 16), 0.0, A.mult, A.add)
        for h in range(2):
            ts(r("EOFF", h, 8, 2), r("C4"), r("UU", 30 + h, 31 + h), A.add, 4.0, A.mult)
        for e in range(2):
            act(r("ET", 2 + e, 128, 4), X, r("EOFF", 4 + 2 * e, 6 + 2 * e))
            copy(r("ET", e, 128, 4), X, r("EOFF", 2 * e, 2 * e + 2))
        QE, QES = r("QE%d" % t), r("QES%d" % t)
        if t == 0:
            ts(r("TL"), r("IL"), col(0), A.is_equal, float(2 ** 20), A.mult)
        quant(QE, QES, r("ET"))
        dst = T.cores[(rank + 1 + t) % N]
        rid, pid = topo.addr(dst)[:2]
        far = min((topo.engines(core, c) for c in T.cores if c != core), key=len)
        eng = [e for e in topo.engines(core, dst) if e in far]
        half = len(eng) // 2
        masks = [sum(1 << e for e in eng[:half]), sum(1 << e for e in eng[half:])]
        arr = "arr%d" % t

        def send():
            to = [DstId(rid=rid, pnc=pid)]
            g.remote_dma_fused([
                RemoteDMATransfer(dst_ids=to, dma_engine_mask=masks[0], remote_sem=T.sem[arr],
                                  src=ap(r(QE[0], 0, 32)).bitcast(dt.uint8), dst=ap(r(TG, 256, 288)).bitcast(dt.uint8)),
                RemoteDMATransfer(dst_ids=to, dma_engine_mask=masks[1], remote_sem=T.sem[arr],
                                  src=ap(QES), dst=ap(r(TS, 256, 384)))], local_sem=T.sem.sent)
        issue("g", send, [QE, QES], [], sem="sent", inc=2 * half)
        count[arr] = 2 * half
        for nm, a, b in ((TG, 256, 288), (TS, 256, 384)):
            log.setdefault(nm, []).append((frozenset(range(a, b)), True, "far", arr, 2 * half, {}))

        def guests():
            gst = (r(TG, 160, 288), r(TS, 160, 288))
            mm(r("PB0", 0, 128), r("QU"), r("QUS"), *gst)
            mm(r("PB1", 0, 128), r("QB"), r("QBS"), *gst)
            for b in range(4):
                mm(r("PA%d" % b, 0, 288), *unit(b, b < NX), r(TG), r(TS, 0, 288))

        if t == 0:
            iota(r("IR"), [[0, 16], [16, 2]], 256)
            for b in range(4):
                mm(r("PA%d" % b, 0, 256), *unit(b, b < NX), *own)
            inverse(guests)
            iota(r("IOT"), [[1, 288]])
        else:
            own_rows()
            unpack_own()
            tr(r("OW", 64), r("VB", 64))
        dealt(r("OW"), "OOFF", "G1", "GT", CUT1)
        if t == 0:
            for l in range(2):
                copy(r("IG", 32 * l, 32 * l + 32), r("GT", 16 * l + 2, 1024, 32))
        for l in range(2):
            (act if t == 0 else copy)(r("CAND", 64 * l + 1, 64 * l + 64, 2), r("GT", 16 * l, 1024, 32))
            if t == 0:
                act(r("CAND", 64 * l, 64 * l + 64, 2), r("GT", 16 * l + 3, 1024, 32))
        if t == 0:
            for k in range(3):
                copy(r("INX", k, 64, 4), r("IG", k + 1, 64, 4))
        for l in range(2):
            so = r("GT", 16 * l + 1, 1024, 32)
            tt(r("DS", 64 * l, 64 * l + 64, 2), r("IG", 32 * l, 32 * l + 32), so, A.subtract)
            tt(r("DS", 64 * l + 1, 64 * l + 64, 2), so, r("INX", 32 * l, 32 * l + 32), A.subtract)

        if t > 0:
            guests()
            act(r("ZW", 0, 32), r("PB0", 96, 128))
            act(r("ZW", 32, 64), r("PB1", 96, 128))
            dealt(r("ZW"), "GOFF", "G2", "GT", CUT2)
            for l in range(2):
                copy(r("CAND", 64 * l, 64 * l + 64, 2), r("GT", 16 * l, 1024, 32))
        for b in range(4):
            act(r("HW", 288 * b + 256, 288 * b + 288), r("PA%d" % b, 256, 288), scale=1.0 if b < NX else 0.5)
        for h in range(2):
            for b in range(NXH[h], 4):
                act(r("HC", 256 * (b - 2) + 128 * h, 256 * (b - 2) + 128 * h + 128), r("PA%d" % b, 128 * h, 128 * h + 128),
                    scale=1.0 if b < NX else 0.5)
        for a in (0, 64):
            scan(r("MX", a + 1, a + 65), r("CAND", a, a + 64), r("SEG8", a, a + 64), LOW, A.max, A.add)
        for a in (0, 64):
            tt(r("NA8", a, a + 64), r("CAND", a, a + 64), r("MX", a, a + 64), A.is_le)
        for a in (0, 64):
            scan(r("UA", a, a + 64), r("NA8", a, a + 64), r("DS", a, a + 64), 0.0, A.mult, A.add)
        for l in range(2):
            copy(r("AOFF", l, 16, 2), r("UA", 64 * l + 7, 64 * l + 64, 8))
        X = r("X1")
        nq, ns = ("TG%d" % (t + 1), "TS%d" % (t + 1)) if t < R - 1 else ("TF", "TFS")
        order = (3, 0, 1, 2)

        def y_part(h, b):
            a = 128 * h
            out = r("YT", 4 * a + b, 4 * a + 512, 4)
            if b < NXH[h]:
                tt(out, r("TP", 256 * b + a, 256 * b + a + 128), r("PA%d" % b, a, a + 128), A.add)
            else:
                tt(out, r("HW", 288 * b, 288 * b + 288), r("HC", 256 * (b - 2) + a, 256 * (b - 2) + a + 128), A.add,
                   r("AOFF", 8 * h, 8 * h + 8))

        def y_layer(h):
            a = 128 * h
            quant(r("QY", a, a + 128), r("QYS", a, a + 128), r("YT", 4 * a, 4 * a + 512))
            for b in order:
                mm(r("PB%d" % b, 0, 128), r("WC", 128 * b, 128 * b + 128), r("WS", 128 * b, 128 * b + 128),
                   r("QY", a, a + 128), r("QYS", a, a + 128))
                act(r("RL", 256 * b + a, 256 * b + a + 128), r("PB%d" % b, 0, 128), func=ACT.Relu, scale=0.03125)

        def x_part(h, b):
            a = 128 * h
            tt(r("X1", 4 * a + b, 4 * a + 512, 4), r("RL", 256 * b + a, 256 * b + a + 128), r("PA%d" % b, a, a + 128), A.add)

        def x_done(h):
            a = 128 * h
            quant(r(nq, a, a + 128), r(ns, a, a + 128), r("X1", 4 * a, 4 * a + 512))
            if t < R - 1:
                scores(nq, ns, a, a + 128, ("PB3", "PB0") if a == 0 else ("PB1", "PB2"), act if a == 0 else copy)
            else:
                bank = r("PB3" if a == 0 else "PB0", 0, 128)
                mm(bank, r("QV"), r("QVS"), r(nq, a, a + 128), r(ns, a, a + 128))
                if a == 0:
                    act(r("YO", 0, 128), bank)
                    dma("y", T.y[:, 0:128], ap(r("YO", 0, 128)), [r("YO", 0, 128)], [])
                    act(r("OAR"), r("IOT"), r("AOFF"))
                    dma("y", T.oa[:], T.OAR[0:128:16, :], [r("OAR")], [])
                else:
                    act(r("YO", 128, 256), bank)

        for h in range(2):
            for b in range(NXH[h]):
                act(r("TP", 256 * b + 128 * h, 256 * b + 128 * h + 128), r("HW", 288 * b, 288 * b + 288),
                    r("AOFF", 8 * h, 8 * h + 8))
        for step in PLAN:
            if step[0] == "y":
                y_part(int(step[1]), int(step[2]))
            elif step[0] == "q":
                y_layer(int(step[1]))
            elif step[0] == "f":
                for b in range(NX):
                    mm(r("PA%d" % b, 0, 256), *unit(b), *own)
            elif step[0] == "x":
                x_part(int(step[1]), int(step[2]))
            else:
                x_done(int(step[1]))

    dma("y", T.oc[:], ap(r("TF")).bitcast(dt.uint8), [r("TF")], [])
    dma("s", T.y[:, 128:256], ap(r("YO", 128, 256)), [r("YO", 128, 256)], [])
    for k in range(4):
        dma("y", T.osc[4 * k:4 * k + 4, :], T.TFS[32 * k:32 * k + 4, :], [r("TFS")], [])
    for sem, n in count.items():
        wait("y", sem, n, {})
